import numpy as np, ml_dtypes
CORES = [1,17,65,89,97,113]
N = 6
import mx_ref
NC = 512
LR = np.float32(0.02325)
BF = ml_dtypes.bfloat16
def cut(t, i, w=512):
    return t[:, w * i:w * i + w]
def tile(rs):
    return np.stack(rs, axis=2).reshape(128, -1).astype(BF)
def pick(b):
    s = np.zeros((128, 128, 4), np.float32)
    s[np.arange(128), np.arange(128), b] = 1.0
    return mx_ref.quantize(s.reshape(128, 512).astype(BF))
def setup_inputs(rng):
    def f(*shape):
        return mx_ref.flush((rng.standard_normal(shape, dtype=np.float32) * np.exp2(rng.integers(-2, 3, shape[:-1] + (1,)))).astype(BF))
    return {"b": f(N, 128, N * 512), "w": f(N, 128, 512), "x": f(N, 128, 4 * NC)}
def setup_inputs_blocks(rng):
    d = setup_inputs(rng)
    for k in ("b", "w", "x"): d[k] = mx_ref.spread(d[k], rng, 2)
    return d
def setup_inputs_wide(rng):
    d = setup_inputs(rng)
    for k in ("b", "w", "x"): d[k] = mx_ref.flush((d[k].astype(np.float32) * np.exp2(rng.integers(-4, 5, (N, 1, 1))).astype(np.float32)).astype(BF))
    return d
def reference(b, w, x, own=None):
    S = [pick(t) for t in range(4)]
    h = np.zeros((N, 128, 512), BF)
    for c in range(N):
        for r in range(N):
            q = mx_ref.quantize(cut(b[r], c))
            P = [mx_ref.matmul(S[t], q) for t in range(4)]
            Z = P if r == 0 else [z + p for z, p in zip(Z, P)]
        h[c] = tile([w[c].astype(np.float32)[:, t::4] - Z[t] * LR for t in range(4)])
    use = h if own is None else own["h"]
    H = [mx_ref.quantize(use[j]) for j in range(N)]
    y = np.zeros((N, 128, N * NC), np.float32)
    for r in range(N):
        qx = mx_ref.quantize(x[r])
        for j in range(N):
            y[r][:, NC * j:NC * j + NC] = mx_ref.matmul(H[j], qx)
    return {"h": h, "y": y}

@@ -1,0 +1,249 @@
+from concourse.bass import DstId, RemoteDMATransfer
+from concourse.mybir import dt, AluOpType, ActivationFunctionType
+
+SIM_CORES = 128
+W = 128
+NB = 6
+NC = 512
+LR = 0.02325
+
+CODES, PLANE = "float8_e4m3fn_x4", "uint8"
+SCRATCH = {
+    "bt": ("sbuf", [128, NB * 4 * W], "bfloat16"),
+    "wt": ("sbuf", [128, 4 * W], "bfloat16"),
+    "xt": ("sbuf", [128, 4 * NC], "bfloat16"),
+    "ones": ("sbuf", [128, W], "bfloat16"),
+    "dg": ("sbuf", [128, 4 * W + 4], "bfloat16"),
+    "sq": ("sbuf", [128, 4 * W], CODES), "ss": ("sbuf", [128, 4 * W], PLANE),
+    "qc1": ("sbuf", [128, NB * W], CODES), "qp1": ("sbuf", [128, NB * W], PLANE),
+    "qc2": ("sbuf", [128, W], CODES), "qp2": ("sbuf", [128, W], PLANE),
+    "xc": ("sbuf", [128, NC], CODES), "xp": ("sbuf", [128, NC], PLANE),
+    "zs": ("sbuf", [128, 4 * W], "float32"),
+    "ht": ("sbuf", [128, 4 * W], "bfloat16"),
+    "yt": ("sbuf", [128, NB * NC], "float32"),
+    "lc1": ("sbuf", [128, NB * W], CODES), "lp1": ("sbuf", [128, NB * W], PLANE),
+    "lc2": ("sbuf", [128, NB * W], CODES), "lp2": ("sbuf", [128, NB * W], PLANE),
+    "hc1": ("sbuf", [128, 2 * W], CODES), "hp1": ("sbuf", [128, 2 * W], PLANE),
+    "hc2": ("sbuf", [128, W], CODES), "hp2": ("sbuf", [128, W], PLANE),
+    "z": ("psum", [128, 4 * 512], "float32"),
+    "p": ("psum", [128, 4 * 512], "float32"),
+}
+SEMAPHORES = (["ld%d" % k for k in range(NB)] + ["lw", "lx", "fill", "sel", "squant", "bq", "zd", "act", "hsum", "hq", "xq",
+              "ym", "yv", "ya", "stored", "sent1", "sent2", "hin1", "hin2", "hout1", "hout2"]
+              + ["a1_%d" % r for r in range(NB)] + ["a2_%d" % r for r in range(NB)])
+
+
+def bits(mask):
+    return [1 << k for k in range(16) if mask >> k & 1]
+
+
+def part(mask, i, n):
+    e = bits(mask)
+    w = len(e) // n
+    return sum(e[i * w:(i + 1) * w])
+
+
+def make_plan(cores, topo):
+    main = [r for r in range(NB) if any(topo.may_write(cores[r], cores[c]) for c in range(NB) if c != r)]
+    lone = [r for r in range(NB) if r not in main][0]
+    L = cores[lone]
+    chipmates = lambda c: [k for k in range(SIM_CORES) if topo.chip(k) == topo.chip(c) and k not in cores]
+    order, calls, early = {}, {}, {}
+
+    def call(core, phase, need, transfers):
+        calls.setdefault(core, []).append((phase, need, transfers))
+
+    def land(r, c, kind, phase):
+        return (cores[c], "l%s%d" % (kind, phase), W * r, "a%d_%d" % (phase, r))
+
+    def at(h, kind, phase):
+        return (h, "h%s%d" % (kind, phase), 0, "hin%d" % phase)
+
+    for i, r in enumerate(main):
+        me, m = cores[r], len(main)
+        pick = [main[(i + k) % m] for k in range(1, m)]
+        d1, d2, e1, e2 = pick
+        order[r] = [lone, e1, e2, d1, d2, r]
+        near = topo.die(me)
+        mates = chipmates(me)
+        owners = [k for k in mates if topo.may_write(k, L) and (topo.die(k) == near) == (i % 2 == 0)]
+        used = owners[:2]
+        far = [k for k in mates if topo.die(k) != near and k not in used]
+        rest = far[2:] + [k for k in mates if topo.die(k) == near and k not in used]
+        helper = {"c": [used[0], far[0], far[1]], "p": [used[1], rest[0], rest[1]]}
+        chip_mask, far_mask = topo.mask(me, far[0]), topo.mask(me, cores[d1])
+        masks = [part(chip_mask, 0, 2), part(chip_mask, 2, 4), part(chip_mask, 3, 4)]
+        for kind in "cp":
+            call(me, 1, 3, [("q" + kind + "1", W * s, W, [at(helper[kind][s], kind, 1)], masks[s]) for s in range(3)])
+        for kind in "cp":
+            call(me, 1, 5, [("q" + kind + "1", W * (3 + s), W, [land(r, d, kind, 1)], part(far_mask, s, 2)) for s, d in enumerate((d1, d2))])
+        for kind in "cp":
+            call(me, 2, None, [("q" + kind + "2", 0, W, [at(h, kind, 2) for h in helper[kind]], chip_mask)])
+        for kind in "cp":
+            call(me, 2, None, [("q" + kind + "2", 0, W, [land(r, d, kind, 2) for d in (d1, d2)], far_mask)])
+        for kind in "cp":
+            for s, d in enumerate((lone, e1, e2)):
+                h = helper[kind][s]
+                for phase in (1, 2):
+                    call(h, phase, None, [("h%s%d" % (kind, phase), 0, W, [land(r, d, kind, phase)], topo.mask(h, cores[d]))])
+        for d in (d1, d2):
+            early[(r, d)] = 0
+        for d in (e1, e2, lone):
+            early[(r, d)] = 1
+    first = main[-1]
+    four = main[:-1]
+    order[lone] = [first] + four + [lone]
+    mates = chipmates(L)
+    own = [k for k in mates if topo.may_write(k, cores[first])]
+    dies = [[k for k in own if topo.die(k) == topo.die(L)], [k for k in own if topo.die(k) != topo.die(L)]]
+    fars = [k for k in range(SIM_CORES) if topo.mates(topo.chip(k), topo.chip(cores[first])) and topo.die(k) == topo.die(L)
+            and topo.may_write(k, cores[first])]
+    assert all(topo.may_write(L, k) for k in fars)
+    out_mask, chip_mask = topo.mask(L, fars[0]), topo.mask(L, own[0])
+    for j, kind in enumerate("cp"):
+        call(L, 1, 1, [("q" + kind + "1", 0, W, [at(fars[j], kind, 1)], out_mask)])
+    for j, kind in enumerate("cp"):
+        call(L, 1, 5, [("q" + kind + "1", W * (1 + 2 * s), 2 * W, [at(dies[s][j], kind, 1)], part(chip_mask, s, 2)) for s in range(2)])
+    for j, kind in enumerate("cp"):
+        call(L, 2, None, [("q" + kind + "2", 0, W, [at(dies[s][j], kind, 2) for s in range(2)], chip_mask & ~out_mask),
+                          ("q" + kind + "2", 0, W, [at(fars[j], kind, 2)], out_mask)])
+    for j, kind in enumerate("cp"):
+        for phase in (1, 2):
+            call(fars[j], phase, None, [("h%s%d" % (kind, phase), 0, W, [land(lone, first, kind, phase)], topo.mask(fars[j], cores[first]))])
+        for s in range(2):
+            h, two = dies[s][j], four[2 * s:2 * s + 2]
+            mask = topo.mask(h, cores[two[0]])
+            call(h, 1, None, [("h%s1" % kind, W * k, W, [land(lone, d, kind, 1)], part(mask, k, 2)) for k, d in enumerate(two)])
+            call(h, 2, None, [("h%s2" % kind, 0, W, [land(lone, d, kind, 2) for d in two], mask)])
+    for d in main:
+        early[(lone, d)] = 2
+    count = {}
+    for core in calls:
+        for phase, need, transfers in calls[core]:
+            for _b, _a, _w, dsts, mask in transfers:
+                for d, _db, _da, sem in dsts:
+                    count[(d, sem)] = count.get((d, sem), 0) + len(bits(mask))
+    arrival = {c: sorted([r for r in range(NB) if r != c], key=lambda r: (early[(r, c)], (r - c) % NB)) for c in range(NB)}
+    return order, calls, count, arrival
+
+
+def rank_program(g, core, T, topo):
+    order, calls, count, arrival = make_plan(list(T.cores), topo)
+    rank = T.rank_of(core)
+    sem = T.sem
+
+    def view(name, a, w):
+        v = T[name][:, a:a + w]
+        return v.bitcast(dt.uint8) if name[1] == "c" else v
+
+    def send(transfers, local):
+        ts, n = [], 0
+        for buf, a, w, dsts, mask in transfers:
+            ids, outs = [], []
+            for d, db, da, s in dsts:
+                rid, pid, _se = topo.addr(d)
+                ids.append(DstId(rid=rid, pnc=pid))
+                outs.append(view(db, da, w))
+            ts.append(RemoteDMATransfer(dst_ids=ids, dma_engine_mask=mask, remote_sem=sem[dsts[0][3]], srcs=[view(buf, a, w)], dsts=outs))
+            n += len(bits(mask))
+        g.remote_dma_fused(ts, local_sem=local)
+        return n
+
+    if rank is None:
+        for phase in (1, 2):
+            mine = [t for ph, _n, t in calls.get(core, []) if ph == phase]
+            if mine:
+                g.wait_ge(sem["hin%d" % phase], count[(core, "hin%d" % phase)])
+                n = sum([send(t, sem["hout%d" % phase]) for t in mine])
+                g.wait_ge(sem["hout%d" % phase], n)
+        return
+
+    ten, vec, act, syn = g.tensor, g.vector, g.scalar, g.sync
+    slots = order[rank]
+    mine = calls[core]
+    total = {ph: sum(len(bits(m)) for p, _n, t in mine if p == ph for _b, _a, _w, _d, m in t) for ph in (1, 2)}
+
+    for k, c in enumerate(slots):
+        (syn, act)[k % 2].dma_start(T.bt[:, 512 * k:512 * k + 512], T.b[:, 512 * c:512 * c + 512]).then_inc(sem["ld%d" % k], 16)
+    act.dma_start(T.wt[:], T.w[:]).then_inc(sem.lw, 16)
+    syn.wait_ge(sem.sent1, total[1])
+    syn.dma_start(T.xt[:], T.x[:]).then_inc(sem.lx, 16)
+
+    g.wait_ge(sem.fill, 2)
+    g.affine_select(T.dg[:, 3:3 + 4 * W:4], T.ones[:], [[-1, W]], AluOpType.is_equal, 0.0, 0, 1).then_inc(sem.sel, 1)
+    have = 0
+    for phase, need, transfers in mine:
+        if phase == 1:
+            if need > have:
+                g.wait_ge(sem.bq, need)
+                have = need
+            send(transfers, sem.sent1)
+    g.wait_ge(sem.hq, 1)
+    for phase, need, transfers in mine:
+        if phase == 2:
+            send(transfers, sem.sent2)
+    g.wait_ge(sem.sent2, total[2])
+
+    vec.memset(T.dg[:], 0.0).then_inc(sem.fill, 1)
+    vec.memset(T.ones[:], 1.0).then_inc(sem.fill, 1)
+    vec.wait_ge(sem.sel, 1)
+    for b in range(4):
+        vec.quantize_mx(T.sq[:, W * b:W * b + W], T.ss[:, W * b:W * b + W], T.dg[:, 3 - b:3 - b + 4 * W]).then_inc(sem.squant, 1)
+    for k in range(NB):
+        vec.wait_ge(sem["ld%d" % k], 16)
+        vec.quantize_mx(T.qc1[:, W * k:W * k + W], T.qp1[:, W * k:W * k + W], T.bt[:, 512 * k:512 * k + 512]).then_inc(sem.bq, 1)
+    vec.wait_ge(sem.lw, 16)
+    for b in range(4):
+        vec.wait_ge(sem.act, b + 1)
+        vec.tensor_tensor(T.ht[:, b:4 * W:4], T.wt[:, b:4 * W:4], T.zs[:, W * b:W * b + W], AluOpType.subtract).then_inc(sem.hsum, 1)
+    vec.wait_ge(sem.hsum, 4)
+    vec.quantize_mx(T.qc2[:], T.qp2[:], T.ht[:]).then_inc(sem.hq, 1)
+    vec.wait_ge(sem.lx, 16)
+    vec.quantize_mx(T.xc[:], T.xp[:], T.xt[:]).then_inc(sem.xq, 1)
+
+    srcs = [rank] + arrival[rank]
+    ten.wait_ge(sem.squant, 4)
+    for k, r in enumerate(srcs):
+        if k == 0:
+            ten.wait_ge(sem.bq, NB)
+            q, s, a = T.qc1, T.qp1, W * (NB - 1)
+        else:
+            ten.wait_ge(sem["a1_%d" % r], count[(core, "a1_%d" % r)])
+            q, s, a = T.lc1, T.lp1, W * r
+        for b in range(4):
+            mm = ten.matmul_mx(T.z[:, 512 * b:512 * b + W], T.sq[:, W * b:W * b + W], T.ss[:, W * b:W * b + W],
+                               q[:, a:a + W], s[:, a:a + W], k == 0, k == NB - 1)
+            if k == NB - 1:
+                mm.then_inc(sem.zd, 1)
+    for b in range(4):
+        act.wait_ge(sem.zd, b + 1)
+        act.activation(T.zs[:, W * b:W * b + W], T.z[:, 512 * b:512 * b + W], ActivationFunctionType.Copy, scale=LR).then_inc(sem.act, 1)
+
+    ten.wait_ge(sem.hq, 1)
+    ten.wait_ge(sem.xq, 1)
+    ten.wait_ge(sem.act, 4)
+    done = [0, 0]
+    for k, j in enumerate(srcs):
+        if k == 0:
+            q, s, a = T.qc2, T.qp2, 0
+        else:
+            ten.wait_ge(sem["a2_%d" % j], count[(core, "a2_%d" % j)])
+            q, s, a = T.lc2, T.lp2, W * j
+        bank = T.p[:, 512 * k:512 * k + NC] if k < 4 else T.z[:, 512 * (k - 4):512 * (k - 4) + NC]
+        ten.matmul_mx(bank, q[:, a:a + W], s[:, a:a + W], T.xc[:], T.xp[:], True, True).then_inc(sem.ym, 1)
+        out = T.yt[:, NC * k:NC * k + NC]
+        e = k % 2
+        done[e] += 1
+        if e == 0:
+            vec.wait_ge(sem.ym, k + 1)
+            vec.tensor_copy(out, bank).then_inc(sem.yv, 1)
+            syn.wait_ge(sem.yv, done[e])
+        else:
+            act.wait_ge(sem.ym, k + 1)
+            act.activation(out, bank, ActivationFunctionType.Copy).then_inc(sem.ya, 1)
+            syn.wait_ge(sem.ya, done[e])
+        syn.dma_start(T.y[:, NC * j:NC * j + NC], out).then_inc(sem.stored, 16)
+        if k == 0:
+            syn.wait_ge(sem.hq, 1)
+            syn.dma_start(T.h[:], T.ht[:]).then_inc(sem.stored, 16)
+    syn.wait_ge(sem.stored, 16 * (NB + 1))

@@ -5,6 +5,8 @@ SIM_CORES = 128
 W = 128
 NB = 6
 NC = 512
+H = NC // 2
+BANK = 512
 LR = 0.02325
 
 CODES, PLANE = "float8_e4m3fn_x4", "uint8"
@@ -25,8 +27,7 @@ SCRATCH = {
     "lc2": ("sbuf", [128, NB * W], CODES), "lp2": ("sbuf", [128, NB * W], PLANE),
     "hc1": ("sbuf", [128, 2 * W], CODES), "hp1": ("sbuf", [128, 2 * W], PLANE),
     "hc2": ("sbuf", [128, W], CODES), "hp2": ("sbuf", [128, W], PLANE),
-    "z": ("psum", [128, 4 * 512], "float32"),
-    "p": ("psum", [128, 4 * 512], "float32"),
+    "ps": ("psum", [128, 8 * BANK], "float32"),
 }
 SEMAPHORES = (["ld%d" % k for k in range(NB)] + ["lw", "lx", "fill", "sel", "squant", "bq", "zd", "act", "hsum", "hq", "xq",
               "ym", "yv", "ya", "stored", "sent1", "sent2", "hin1", "hin2", "hout1", "hout2"]
@@ -48,7 +49,7 @@ def make_plan(cores, topo):
     lone = [r for r in range(NB) if r not in main][0]
     L = cores[lone]
     chipmates = lambda c: [k for k in range(SIM_CORES) if topo.chip(k) == topo.chip(c) and k not in cores]
-    order, calls, early = {}, {}, {}
+    order, calls, due = {}, {}, {}
 
     def call(core, phase, need, transfers):
         calls.setdefault(core, []).append((phase, need, transfers))
@@ -59,54 +60,61 @@ def make_plan(cores, topo):
     def at(h, kind, phase):
         return (h, "h%s%d" % (kind, phase), 0, "hin%d" % phase)
 
+    def one(kind, slot, dst, mask):
+        return ("q%s1" % kind, W * slot, W, [dst], mask)
+
+    def new(kind, dsts, mask):
+        return ("q%s2" % kind, 0, W, dsts, mask)
+
     for i, r in enumerate(main):
         me, m = cores[r], len(main)
-        pick = [main[(i + k) % m] for k in range(1, m)]
-        d1, d2, e1, e2 = pick
-        order[r] = [lone, e1, e2, d1, d2, r]
+        d1, d2, e1, e2 = [main[(i + k) % m] for k in range(1, m)]
+        order[r] = [lone, e1, d1, e2, d2, r]
         near = topo.die(me)
         mates = chipmates(me)
-        owners = [k for k in mates if topo.may_write(k, L) and (topo.die(k) == near) == (i % 2 == 0)]
-        used = owners[:2]
+        used = [k for k in mates if topo.may_write(k, L) and (topo.die(k) == near) == (i % 2 == 0)][:2]
         far = [k for k in mates if topo.die(k) != near and k not in used]
         rest = far[2:] + [k for k in mates if topo.die(k) == near and k not in used]
         helper = {"c": [used[0], far[0], far[1]], "p": [used[1], rest[0], rest[1]]}
-        chip_mask, far_mask = topo.mask(me, far[0]), topo.mask(me, cores[d1])
-        masks = [part(chip_mask, 0, 2), part(chip_mask, 2, 4), part(chip_mask, 3, 4)]
+        chip_mask, out_mask = topo.mask(me, far[0]), topo.mask(me, cores[d1])
+        in_mask = chip_mask & ~out_mask
         for kind in "cp":
-            call(me, 1, 3, [("q" + kind + "1", W * s, W, [at(helper[kind][s], kind, 1)], masks[s]) for s in range(3)])
+            call(me, 1, 1, [one(kind, 0, at(helper[kind][0], kind, 1), chip_mask)])
+        for s, d in ((1, d1), (2, d2)):
+            for kind in "cp":
+                call(me, 1, 2 * s + 1, [one(kind, 2 * s - 1, at(helper[kind][s], kind, 1), in_mask),
+                                        one(kind, 2 * s, land(r, d, kind, 1), out_mask)])
         for kind in "cp":
-            call(me, 1, 5, [("q" + kind + "1", W * (3 + s), W, [land(r, d, kind, 1)], part(far_mask, s, 2)) for s, d in enumerate((d1, d2))])
+            call(me, 2, None, [new(kind, [at(helper[kind][0], kind, 2)], chip_mask)])
         for kind in "cp":
-            call(me, 2, None, [("q" + kind + "2", 0, W, [at(h, kind, 2) for h in helper[kind]], chip_mask)])
-        for kind in "cp":
-            call(me, 2, None, [("q" + kind + "2", 0, W, [land(r, d, kind, 2) for d in (d1, d2)], far_mask)])
+            call(me, 2, None, [new(kind, [at(helper[kind][1], kind, 2)], in_mask),
+                               new(kind, [land(r, d, kind, 2) for d in (d1, d2)], out_mask)])
         for kind in "cp":
             for s, d in enumerate((lone, e1, e2)):
                 h = helper[kind][s]
-                for phase in (1, 2):
-                    call(h, phase, None, [("h%s%d" % (kind, phase), 0, W, [land(r, d, kind, phase)], topo.mask(h, cores[d]))])
-        for d in (d1, d2):
-            early[(r, d)] = 0
-        for d in (e1, e2, lone):
-            early[(r, d)] = 1
-    first = main[-1]
-    four = main[:-1]
+                call(h, 1, None, [("h%s1" % kind, 0, W, [land(r, d, kind, 1)], topo.mask(h, cores[d]))])
+            for s, ds in enumerate(((lone,), (e1, e2))):
+                h = helper[kind][s]
+                call(h, 2, None, [("h%s2" % kind, 0, W, [land(r, d, kind, 2) for d in ds], topo.mask(h, cores[ds[0]]))])
+        for n, d in enumerate((d1, d2, e1, e2)):
+            due[(r, d)] = n
+        due[(r, lone)] = 1 - i % 2
+    first, four = main[-1], main[:-1]
     order[lone] = [first] + four + [lone]
-    mates = chipmates(L)
-    own = [k for k in mates if topo.may_write(k, cores[first])]
+    own = [k for k in chipmates(L) if topo.may_write(k, cores[first])]
     dies = [[k for k in own if topo.die(k) == topo.die(L)], [k for k in own if topo.die(k) != topo.die(L)]]
     fars = [k for k in range(SIM_CORES) if topo.mates(topo.chip(k), topo.chip(cores[first])) and topo.die(k) == topo.die(L)
-            and topo.may_write(k, cores[first])]
-    assert all(topo.may_write(L, k) for k in fars)
-    out_mask, chip_mask = topo.mask(L, fars[0]), topo.mask(L, own[0])
+            and topo.may_write(k, cores[first]) and topo.may_write(L, k)]
+    chip_mask, out_mask = topo.mask(L, own[0]), topo.mask(L, fars[0])
+    in_mask = chip_mask & ~out_mask
     for j, kind in enumerate("cp"):
-        call(L, 1, 1, [("q" + kind + "1", 0, W, [at(fars[j], kind, 1)], out_mask)])
+        call(L, 1, 1, [one(kind, 0, at(fars[j], kind, 1), out_mask)])
+    for s in range(2):
+        for j, kind in enumerate("cp"):
+            call(L, 1, 3 + 2 * s, [("q%s1" % kind, W * (1 + 2 * s), 2 * W, [at(dies[s][j], kind, 1)], in_mask)])
     for j, kind in enumerate("cp"):
-        call(L, 1, 5, [("q" + kind + "1", W * (1 + 2 * s), 2 * W, [at(dies[s][j], kind, 1)], part(chip_mask, s, 2)) for s in range(2)])
-    for j, kind in enumerate("cp"):
-        call(L, 2, None, [("q" + kind + "2", 0, W, [at(dies[s][j], kind, 2) for s in range(2)], chip_mask & ~out_mask),
-                          ("q" + kind + "2", 0, W, [at(fars[j], kind, 2)], out_mask)])
+        call(L, 2, None, [new(kind, [at(dies[s][j], kind, 2) for s in range(2)], in_mask),
+                          new(kind, [at(fars[j], kind, 2)], out_mask)])
     for j, kind in enumerate("cp"):
         for phase in (1, 2):
             call(fars[j], phase, None, [("h%s%d" % (kind, phase), 0, W, [land(lone, first, kind, phase)], topo.mask(fars[j], cores[first]))])
@@ -116,14 +124,14 @@ def make_plan(cores, topo):
             call(h, 1, None, [("h%s1" % kind, W * k, W, [land(lone, d, kind, 1)], part(mask, k, 2)) for k, d in enumerate(two)])
             call(h, 2, None, [("h%s2" % kind, 0, W, [land(lone, d, kind, 2) for d in two], mask)])
     for d in main:
-        early[(lone, d)] = 2
+        due[(lone, d)] = NB
     count = {}
     for core in calls:
         for phase, need, transfers in calls[core]:
             for _b, _a, _w, dsts, mask in transfers:
                 for d, _db, _da, sem in dsts:
                     count[(d, sem)] = count.get((d, sem), 0) + len(bits(mask))
-    arrival = {c: sorted([r for r in range(NB) if r != c], key=lambda r: (early[(r, c)], (r - c) % NB)) for c in range(NB)}
+    arrival = {c: sorted([r for r in range(NB) if r != c], key=lambda r: (due[(r, c)], r)) for c in range(NB)}
     return order, calls, count, arrival
 
 
@@ -163,8 +171,12 @@ def rank_program(g, core, T, topo):
     mine = calls[core]
     total = {ph: sum(len(bits(m)) for p, _n, t in mine if p == ph for _b, _a, _w, _d, m in t) for ph in (1, 2)}
 
-    for k, c in enumerate(slots):
-        (syn, act)[k % 2].dma_start(T.bt[:, 512 * k:512 * k + 512], T.b[:, 512 * c:512 * c + 512]).then_inc(sem["ld%d" % k], 16)
+    for e in range(2):
+        (syn, act)[e].dma_start(T.bt[64 * e:64 * e + 64, 0:4 * W],
+                                T.b[64 * e:64 * e + 64, 4 * W * slots[0]:4 * W * slots[0] + 4 * W]).then_inc(sem.ld0, 16)
+    for k in range(1, NB):
+        a, c = 4 * W * k, 4 * W * slots[k]
+        (syn, act)[k % 2].dma_start(T.bt[:, a:a + 4 * W], T.b[:, c:c + 4 * W]).then_inc(sem["ld%d" % k], 16)
     act.dma_start(T.wt[:], T.w[:]).then_inc(sem.lw, 16)
     syn.wait_ge(sem.sent1, total[1])
     syn.dma_start(T.xt[:], T.x[:]).then_inc(sem.lx, 16)
@@ -186,12 +198,13 @@ def rank_program(g, core, T, topo):
 
     vec.memset(T.dg[:], 0.0).then_inc(sem.fill, 1)
     vec.memset(T.ones[:], 1.0).then_inc(sem.fill, 1)
-    vec.wait_ge(sem.sel, 1)
-    for b in range(4):
-        vec.quantize_mx(T.sq[:, W * b:W * b + W], T.ss[:, W * b:W * b + W], T.dg[:, 3 - b:3 - b + 4 * W]).then_inc(sem.squant, 1)
     for k in range(NB):
-        vec.wait_ge(sem["ld%d" % k], 16)
-        vec.quantize_mx(T.qc1[:, W * k:W * k + W], T.qp1[:, W * k:W * k + W], T.bt[:, 512 * k:512 * k + 512]).then_inc(sem.bq, 1)
+        if k == NB - 1:
+            vec.wait_ge(sem.sel, 1)
+            for b in range(4):
+                vec.quantize_mx(T.sq[:, W * b:W * b + W], T.ss[:, W * b:W * b + W], T.dg[:, 3 - b:3 - b + 4 * W]).then_inc(sem.squant, 1)
+        vec.wait_ge(sem["ld%d" % k], 32 if k == 0 else 16)
+        vec.quantize_mx(T.qc1[:, W * k:W * k + W], T.qp1[:, W * k:W * k + W], T.bt[:, 4 * W * k:4 * W * k + 4 * W]).then_inc(sem.bq, 1)
     vec.wait_ge(sem.lw, 16)
     for b in range(4):
         vec.wait_ge(sem.act, b + 1)
@@ -211,39 +224,41 @@ def rank_program(g, core, T, topo):
             ten.wait_ge(sem["a1_%d" % r], count[(core, "a1_%d" % r)])
             q, s, a = T.lc1, T.lp1, W * r
         for b in range(4):
-            mm = ten.matmul_mx(T.z[:, 512 * b:512 * b + W], T.sq[:, W * b:W * b + W], T.ss[:, W * b:W * b + W],
+            mm = ten.matmul_mx(T.ps[:, BANK * b:BANK * b + W], T.sq[:, W * b:W * b + W], T.ss[:, W * b:W * b + W],
                                q[:, a:a + W], s[:, a:a + W], k == 0, k == NB - 1)
             if k == NB - 1:
                 mm.then_inc(sem.zd, 1)
     for b in range(4):
         act.wait_ge(sem.zd, b + 1)
-        act.activation(T.zs[:, W * b:W * b + W], T.z[:, 512 * b:512 * b + W], ActivationFunctionType.Copy, scale=LR).then_inc(sem.act, 1)
+        act.activation(T.zs[:, W * b:W * b + W], T.ps[:, BANK * b:BANK * b + W], ActivationFunctionType.Copy, scale=LR).then_inc(sem.act, 1)
 
     ten.wait_ge(sem.hq, 1)
     ten.wait_ge(sem.xq, 1)
     ten.wait_ge(sem.act, 4)
-    done = [0, 0]
+    syn.wait_ge(sem.hq, 1)
+    syn.wait_ge(sem.sent2, total[2])
+    syn.dma_start(T.h[:], T.ht[:]).then_inc(sem.stored, 16)
     for k, j in enumerate(srcs):
         if k == 0:
             q, s, a = T.qc2, T.qp2, 0
         else:
             ten.wait_ge(sem["a2_%d" % j], count[(core, "a2_%d" % j)])
             q, s, a = T.lc2, T.lp2, W * j
-        bank = T.p[:, 512 * k:512 * k + NC] if k < 4 else T.z[:, 512 * (k - 4):512 * (k - 4) + NC]
-        ten.matmul_mx(bank, q[:, a:a + W], s[:, a:a + W], T.xc[:], T.xp[:], True, True).then_inc(sem.ym, 1)
-        out = T.yt[:, NC * k:NC * k + NC]
-        e = k % 2
-        done[e] += 1
-        if e == 0:
-            vec.wait_ge(sem.ym, k + 1)
-            vec.tensor_copy(out, bank).then_inc(sem.yv, 1)
-            syn.wait_ge(sem.yv, done[e])
-        else:
-            act.wait_ge(sem.ym, k + 1)
-            act.activation(out, bank, ActivationFunctionType.Copy).then_inc(sem.ya, 1)
-            syn.wait_ge(sem.ya, done[e])
-        syn.dma_start(T.y[:, NC * j:NC * j + NC], out).then_inc(sem.stored, 16)
-        if k == 0:
-            syn.wait_ge(sem.hq, 1)
-            syn.dma_start(T.h[:], T.ht[:]).then_inc(sem.stored, 16)
+        if k >= 4:
+            ten.wait_ge(sem.yv, k - 3)
+            ten.wait_ge(sem.ya, k - 3)
+        for e in range(2):
+            n = (4 + 2 * k + e) % 8
+            bank = T.ps[:, BANK * n:BANK * n + H]
+            out = T.yt[:, NC * k + H * e:NC * k + H * e + H]
+            ten.matmul_mx(bank, q[:, a:a + W], s[:, a:a + W], T.xc[:, H * e:H * e + H], T.xp[:, H * e:H * e + H], True, True).then_inc(sem.ym, 1)
+            if e == 0:
+                vec.wait_ge(sem.ym, 2 * k + 1)
+                vec.tensor_copy(out, bank).then_inc(sem.yv, 1)
+            else:
+                act.wait_ge(sem.ym, 2 * k + 2)
+                act.activation(out, bank, ActivationFunctionType.Copy).then_inc(sem.ya, 1)
+        syn.wait_ge(sem.yv, k + 1)
+        syn.wait_ge(sem.ya, k + 1)
+        syn.dma_start(T.y[:, NC * j:NC * j + NC], T.yt[:, NC * k:NC * k + NC]).then_inc(sem.stored, 16)
     syn.wait_ge(sem.stored, 16 * (NB + 1))

from concourse.bass import DstId, RemoteDMATransfer
from concourse.mybir import dt, AluOpType, ActivationFunctionType

SIM_CORES = 128
W = 128
NB = 6
NC = 512
H = NC // 2
BANK = 512
LR = 0.02325

CODES, PLANE = "float8_e4m3fn_x4", "uint8"
SCRATCH = {
    "bt": ("sbuf", [128, NB * 4 * W], "bfloat16"),
    "wt": ("sbuf", [128, 4 * W], "bfloat16"),
    "xt": ("sbuf", [128, 4 * NC], "bfloat16"),
    "ones": ("sbuf", [128, W], "bfloat16"),
    "dg": ("sbuf", [128, 4 * W + 4], "bfloat16"),
    "sq": ("sbuf", [128, 4 * W], CODES), "ss": ("sbuf", [128, 4 * W], PLANE),
    "qc1": ("sbuf", [128, NB * W], CODES), "qp1": ("sbuf", [128, NB * W], PLANE),
    "qc2": ("sbuf", [128, W], CODES), "qp2": ("sbuf", [128, W], PLANE),
    "xc": ("sbuf", [128, NC], CODES), "xp": ("sbuf", [128, NC], PLANE),
    "zs": ("sbuf", [128, 4 * W], "float32"),
    "ht": ("sbuf", [128, 4 * W], "bfloat16"),
    "yt": ("sbuf", [128, NB * NC], "float32"),
    "lc1": ("sbuf", [128, NB * W], CODES), "lp1": ("sbuf", [128, NB * W], PLANE),
    "lc2": ("sbuf", [128, NB * W], CODES), "lp2": ("sbuf", [128, NB * W], PLANE),
    "hc1": ("sbuf", [128, 2 * W], CODES), "hp1": ("sbuf", [128, 2 * W], PLANE),
    "hc2": ("sbuf", [128, W], CODES), "hp2": ("sbuf", [128, W], PLANE),
    "ps": ("psum", [128, 8 * BANK], "float32"),
}
SEMAPHORES = (["ld%d" % k for k in range(NB)] + ["lw", "lx", "fill", "sel", "squant", "bq", "zd", "act", "hsum", "hq", "xq",
              "ym", "yv", "ya", "stored", "sent1", "sent2", "hin1", "hin2", "hout1", "hout2"]
              + ["a1_%d" % r for r in range(NB)] + ["a2_%d" % r for r in range(NB)])


def bits(mask):
    return [1 << k for k in range(16) if mask >> k & 1]


def part(mask, i, n):
    e = bits(mask)
    w = len(e) // n
    return sum(e[i * w:(i + 1) * w])


def make_plan(cores, topo):
    main = [r for r in range(NB) if any(topo.may_write(cores[r], cores[c]) for c in range(NB) if c != r)]
    lone = [r for r in range(NB) if r not in main][0]
    L = cores[lone]
    chipmates = lambda c: [k for k in range(SIM_CORES) if topo.chip(k) == topo.chip(c) and k not in cores]
    order, calls, due = {}, {}, {}

    def call(core, phase, need, transfers):
        calls.setdefault(core, []).append((phase, need, transfers))

    def land(r, c, kind, phase):
        return (cores[c], "l%s%d" % (kind, phase), W * r, "a%d_%d" % (phase, r))

    def at(h, kind, phase):
        return (h, "h%s%d" % (kind, phase), 0, "hin%d" % phase)

    def one(kind, slot, dst, mask):
        return ("q%s1" % kind, W * slot, W, [dst], mask)

    def new(kind, dsts, mask):
        return ("q%s2" % kind, 0, W, dsts, mask)

    for i, r in enumerate(main):
        me, m = cores[r], len(main)
        d1, d2, e1, e2 = [main[(i + k) % m] for k in range(1, m)]
        order[r] = [lone, e1, d1, e2, d2, r]
        near = topo.die(me)
        mates = chipmates(me)
        used = [k for k in mates if topo.may_write(k, L) and (topo.die(k) == near) == (i % 2 == 0)][:2]
        far = [k for k in mates if topo.die(k) != near and k not in used]
        rest = far[2:] + [k for k in mates if topo.die(k) == near and k not in used]
        helper = {"c": [used[0], far[0], far[1]], "p": [used[1], rest[0], rest[1]]}
        chip_mask, out_mask = topo.mask(me, far[0]), topo.mask(me, cores[d1])
        in_mask = chip_mask & ~out_mask
        for kind in "cp":
            call(me, 1, 1, [one(kind, 0, at(helper[kind][0], kind, 1), chip_mask)])
        for s, d in ((1, d1), (2, d2)):
            for kind in "cp":
                call(me, 1, 2 * s + 1, [one(kind, 2 * s - 1, at(helper[kind][s], kind, 1), in_mask),
                                        one(kind, 2 * s, land(r, d, kind, 1), out_mask)])
        for kind in "cp":
            call(me, 2, None, [new(kind, [at(helper[kind][0], kind, 2)], chip_mask)])
        for kind in "cp":
            call(me, 2, None, [new(kind, [at(helper[kind][1], kind, 2)], in_mask),
                               new(kind, [land(r, d, kind, 2) for d in (d1, d2)], out_mask)])
        for kind in "cp":
            for s, d in enumerate((lone, e1, e2)):
                h = helper[kind][s]
                call(h, 1, None, [("h%s1" % kind, 0, W, [land(r, d, kind, 1)], topo.mask(h, cores[d]))])
            for s, ds in enumerate(((lone,), (e1, e2))):
                h = helper[kind][s]
                call(h, 2, None, [("h%s2" % kind, 0, W, [land(r, d, kind, 2) for d in ds], topo.mask(h, cores[ds[0]]))])
        for n, d in enumerate((d1, d2, e1, e2)):
            due[(r, d)] = n
        due[(r, lone)] = 1 - i % 2
    first, four = main[-1], main[:-1]
    order[lone] = [first] + four + [lone]
    own = [k for k in chipmates(L) if topo.may_write(k, cores[first])]
    dies = [[k for k in own if topo.die(k) == topo.die(L)], [k for k in own if topo.die(k) != topo.die(L)]]
    fars = [k for k in range(SIM_CORES) if topo.mates(topo.chip(k), topo.chip(cores[first])) and topo.die(k) == topo.die(L)
            and topo.may_write(k, cores[first]) and topo.may_write(L, k)]
    chip_mask, out_mask = topo.mask(L, own[0]), topo.mask(L, fars[0])
    in_mask = chip_mask & ~out_mask
    for j, kind in enumerate("cp"):
        call(L, 1, 1, [one(kind, 0, at(fars[j], kind, 1), out_mask)])
    for s in range(2):
        for j, kind in enumerate("cp"):
            call(L, 1, 3 + 2 * s, [("q%s1" % kind, W * (1 + 2 * s), 2 * W, [at(dies[s][j], kind, 1)], in_mask)])
    for j, kind in enumerate("cp"):
        call(L, 2, None, [new(kind, [at(dies[s][j], kind, 2) for s in range(2)], in_mask),
                          new(kind, [at(fars[j], kind, 2)], out_mask)])
    for j, kind in enumerate("cp"):
        for phase in (1, 2):
            call(fars[j], phase, None, [("h%s%d" % (kind, phase), 0, W, [land(lone, first, kind, phase)], topo.mask(fars[j], cores[first]))])
        for s in range(2):
            h, two = dies[s][j], four[2 * s:2 * s + 2]
            mask = topo.mask(h, cores[two[0]])
            call(h, 1, None, [("h%s1" % kind, W * k, W, [land(lone, d, kind, 1)], part(mask, k, 2)) for k, d in enumerate(two)])
            call(h, 2, None, [("h%s2" % kind, 0, W, [land(lone, d, kind, 2) for d in two], mask)])
    for d in main:
        due[(lone, d)] = NB
    count = {}
    for core in calls:
        for phase, need, transfers in calls[core]:
            for _b, _a, _w, dsts, mask in transfers:
                for d, _db, _da, sem in dsts:
                    count[(d, sem)] = count.get((d, sem), 0) + len(bits(mask))
    arrival = {c: sorted([r for r in range(NB) if r != c], key=lambda r: (due[(r, c)], r)) for c in range(NB)}
    return order, calls, count, arrival


def rank_program(g, core, T, topo):
    order, calls, count, arrival = make_plan(list(T.cores), topo)
    rank = T.rank_of(core)
    sem = T.sem

    def view(name, a, w):
        v = T[name][:, a:a + w]
        return v.bitcast(dt.uint8) if name[1] == "c" else v

    def send(transfers, local):
        ts, n = [], 0
        for buf, a, w, dsts, mask in transfers:
            ids, outs = [], []
            for d, db, da, s in dsts:
                rid, pid, _se = topo.addr(d)
                ids.append(DstId(rid=rid, pnc=pid))
                outs.append(view(db, da, w))
            ts.append(RemoteDMATransfer(dst_ids=ids, dma_engine_mask=mask, remote_sem=sem[dsts[0][3]], srcs=[view(buf, a, w)], dsts=outs))
            n += len(bits(mask))
        g.remote_dma_fused(ts, local_sem=local)
        return n

    if rank is None:
        for phase in (1, 2):
            mine = [t for ph, _n, t in calls.get(core, []) if ph == phase]
            if mine:
                g.wait_ge(sem["hin%d" % phase], count[(core, "hin%d" % phase)])
                n = sum([send(t, sem["hout%d" % phase]) for t in mine])
                g.wait_ge(sem["hout%d" % phase], n)
        return

    ten, vec, act, syn = g.tensor, g.vector, g.scalar, g.sync
    slots = order[rank]
    mine = calls[core]
    total = {ph: sum(len(bits(m)) for p, _n, t in mine if p == ph for _b, _a, _w, _d, m in t) for ph in (1, 2)}

    for e in range(2):
        (syn, act)[e].dma_start(T.bt[64 * e:64 * e + 64, 0:4 * W],
                                T.b[64 * e:64 * e + 64, 4 * W * slots[0]:4 * W * slots[0] + 4 * W]).then_inc(sem.ld0, 16)
    for k in range(1, NB):
        a, c = 4 * W * k, 4 * W * slots[k]
        (syn, act)[k % 2].dma_start(T.bt[:, a:a + 4 * W], T.b[:, c:c + 4 * W]).then_inc(sem["ld%d" % k], 16)
    act.dma_start(T.wt[:], T.w[:]).then_inc(sem.lw, 16)
    syn.wait_ge(sem.sent1, total[1])
    syn.dma_start(T.xt[:], T.x[:]).then_inc(sem.lx, 16)

    g.wait_ge(sem.fill, 2)
    g.affine_select(T.dg[:, 3:3 + 4 * W:4], T.ones[:], [[-1, W]], AluOpType.is_equal, 0.0, 0, 1).then_inc(sem.sel, 1)
    have = 0
    for phase, need, transfers in mine:
        if phase == 1:
            if need > have:
                g.wait_ge(sem.bq, need)
                have = need
            send(transfers, sem.sent1)
    g.wait_ge(sem.hq, 1)
    for phase, need, transfers in mine:
        if phase == 2:
            send(transfers, sem.sent2)
    g.wait_ge(sem.sent2, total[2])

    vec.memset(T.dg[:], 0.0).then_inc(sem.fill, 1)
    vec.memset(T.ones[:], 1.0).then_inc(sem.fill, 1)
    for k in range(NB):
        if k == NB - 1:
            vec.wait_ge(sem.sel, 1)
            for b in range(4):
                vec.quantize_mx(T.sq[:, W * b:W * b + W], T.ss[:, W * b:W * b + W], T.dg[:, 3 - b:3 - b + 4 * W]).then_inc(sem.squant, 1)
        vec.wait_ge(sem["ld%d" % k], 32 if k == 0 else 16)
        vec.quantize_mx(T.qc1[:, W * k:W * k + W], T.qp1[:, W * k:W * k + W], T.bt[:, 4 * W * k:4 * W * k + 4 * W]).then_inc(sem.bq, 1)
    vec.wait_ge(sem.lw, 16)
    for b in range(4):
        vec.wait_ge(sem.act, b + 1)
        vec.tensor_tensor(T.ht[:, b:4 * W:4], T.wt[:, b:4 * W:4], T.zs[:, W * b:W * b + W], AluOpType.subtract).then_inc(sem.hsum, 1)
    vec.wait_ge(sem.hsum, 4)
    vec.quantize_mx(T.qc2[:], T.qp2[:], T.ht[:]).then_inc(sem.hq, 1)
    vec.wait_ge(sem.lx, 16)
    vec.quantize_mx(T.xc[:], T.xp[:], T.xt[:]).then_inc(sem.xq, 1)

    srcs = [rank] + arrival[rank]
    ten.wait_ge(sem.squant, 4)
    for k, r in enumerate(srcs):
        if k == 0:
            ten.wait_ge(sem.bq, NB)
            q, s, a = T.qc1, T.qp1, W * (NB - 1)
        else:
            ten.wait_ge(sem["a1_%d" % r], count[(core, "a1_%d" % r)])
            q, s, a = T.lc1, T.lp1, W * r
        for b in range(4):
            mm = ten.matmul_mx(T.ps[:, BANK * b:BANK * b + W], T.sq[:, W * b:W * b + W], T.ss[:, W * b:W * b + W],
                               q[:, a:a + W], s[:, a:a + W], k == 0, k == NB - 1)
            if k == NB - 1:
                mm.then_inc(sem.zd, 1)
    for b in range(4):
        act.wait_ge(sem.zd, b + 1)
        act.activation(T.zs[:, W * b:W * b + W], T.ps[:, BANK * b:BANK * b + W], ActivationFunctionType.Copy, scale=LR).then_inc(sem.act, 1)

    ten.wait_ge(sem.hq, 1)
    ten.wait_ge(sem.xq, 1)
    ten.wait_ge(sem.act, 4)
    syn.wait_ge(sem.hq, 1)
    syn.wait_ge(sem.sent2, total[2])
    syn.dma_start(T.h[:], T.ht[:]).then_inc(sem.stored, 16)
    for k, j in enumerate(srcs):
        if k == 0:
            q, s, a = T.qc2, T.qp2, 0
        else:
            ten.wait_ge(sem["a2_%d" % j], count[(core, "a2_%d" % j)])
            q, s, a = T.lc2, T.lp2, W * j
        if k >= 4:
            ten.wait_ge(sem.yv, k - 3)
            ten.wait_ge(sem.ya, k - 3)
        for e in range(2):
            n = (4 + 2 * k + e) % 8
            bank = T.ps[:, BANK * n:BANK * n + H]
            out = T.yt[:, NC * k + H * e:NC * k + H * e + H]
            ten.matmul_mx(bank, q[:, a:a + W], s[:, a:a + W], T.xc[:, H * e:H * e + H], T.xp[:, H * e:H * e + H], True, True).then_inc(sem.ym, 1)
            if e == 0:
                vec.wait_ge(sem.ym, 2 * k + 1)
                vec.tensor_copy(out, bank).then_inc(sem.yv, 1)
            else:
                act.wait_ge(sem.ym, 2 * k + 2)
                act.activation(out, bank, ActivationFunctionType.Copy).then_inc(sem.ya, 1)
        syn.wait_ge(sem.yv, k + 1)
        syn.wait_ge(sem.ya, k + 1)
        syn.dma_start(T.y[:, NC * j:NC * j + NC], T.yt[:, NC * k:NC * k + NC]).then_inc(sem.stored, 16)
    syn.wait_ge(sem.stored, 16 * (NB + 1))
